import numpy as np, ml_dtypes
CORES = [29,45,93,109,157,173,221,237,285,301,349,365,413,429,477,493]
N = 16
QP = 64
def setup_inputs(rng):
    return {"q": rng.standard_normal((N, 128, QP), dtype=np.float32).astype(ml_dtypes.bfloat16), "k": rng.standard_normal((N, 128, 128), dtype=np.float32).astype(ml_dtypes.bfloat16), "v": rng.standard_normal((N, 128, 128), dtype=np.float32).astype(ml_dtypes.bfloat16), "b": (8 * rng.standard_normal((N, 128, N * QP), dtype=np.float32)).astype(ml_dtypes.bfloat16)}
def setup_inputs_big(rng):
    d = setup_inputs(rng)
    for k in ("q", "k", "v", "b"): d[k] = (d[k].astype(np.float32) * 1024.0).astype(d[k].dtype)
    return d
def setup_inputs_small(rng):
    d = setup_inputs(rng)
    for k in ("q", "k", "v", "b"): d[k] = (d[k].astype(np.float32) * (1 / 1024.0)).astype(d[k].dtype)
    return d
def setup_inputs_apart(rng):
    d = setup_inputs(rng)
    f = (10.0 ** rng.permutation(np.linspace(-1.5, 1.5, N))).astype(np.float32).reshape(N, 1, 1)
    for k in ("q", "k", "v", "b"): d[k] = (d[k].astype(np.float32) * f).astype(d[k].dtype)
    return d
def reference(q, k, v, b):
    Q, K, V, B = q.astype(np.float64), k.astype(np.float64), v.astype(np.float64), b.astype(np.float64)
    y = np.zeros((N, 128, QP))
    for r in range(N):
        for j in range(N):
            y[r] += V[j].T @ np.maximum(K[j].T @ Q[r] + B[r][:, QP * j:QP * j + QP], 0.0)
    return {"y": y.astype(ml_dtypes.bfloat16 if q.dtype != np.float64 else np.float64)}

@@ -1,0 +1,176 @@
+from concourse.bass import DstId, RemoteDMATransfer
+from concourse.mybir import AluOpType
+
+QP = 64
+KV = 256
+G = 4
+W = QP * (1 + G)
+
+SCRATCH = {
+    "kv": ("sbuf", [128, G * KV], "bfloat16"),
+    "bs": ("sbuf", [128, 16 * QP], "bfloat16"),
+    "qs": ("sbuf", [128, QP], "bfloat16"),
+    "ob": ("sbuf", [128, 3 * W], "bfloat16"),
+    "ib": ("sbuf", [128, 3 * W], "bfloat16"),
+    "zz": ("sbuf", [128, G * QP], "bfloat16"),
+    "ss": ("sbuf", [128, 4 * G * QP], "bfloat16"),
+    "og": ("sbuf", [128, 3 * QP], "bfloat16"),
+    "oi": ("sbuf", [128, 3 * QP], "bfloat16"),
+    "ys": ("sbuf", [128, QP], "bfloat16"),
+    "p0": ("psum", [128, 512], "float32"),
+    "p1": ("psum", [128, 512], "float32"),
+    "p2": ("psum", [128, 512], "float32"),
+    "p3": ("psum", [128, 512], "float32"),
+}
+SEMAPHORES = (["ld_kv", "ld_qb", "zs", "sent", "vy", "st", "a1", "a2"]
+              + ["kv%d" % i for i in range(G)]
+              + ["%s%d" % (n, i) for n in ("ps", "va", "vr", "po") for i in range(4)]
+              + ["%s%d" % (n, i) for n in ("ob", "bi", "vc", "oi") for i in range(1, 4)])
+
+
+def _layout(T, topo):
+    cols = sorted({topo.chip(c) for c in T.cores})
+    at = {(topo.host(c), cols.index(topo.chip(c))): c for c in T.cores}
+    return cols, at
+
+
+def _place(core, T, topo):
+    cols, at = _layout(T, topo)
+    h, col = topo.host(core), cols.index(topo.chip(core))
+    others = sorted({topo.host(c) for c in T.cores} - {h})
+    near = [x for x in others if topo.rack(x) == topo.rack(h)][0]
+    far = [x for x in others if topo.rack(x) != topo.rack(h) and topo.may_write(core, at[(x, col)])][0]
+    return h, col, near, far
+
+
+def _group(core, T, topo):
+    _, at = _layout(T, topo)
+    h, col, _, far = _place(core, T, topo)
+    first = col - col % 2
+    return sorted((at[(x, c)] for x in (h, far) for c in (first, first + 1)), key=T.rank_of)
+
+
+def _peers(core, T, topo):
+    cols, at = _layout(T, topo)
+    h, col, near, _ = _place(core, T, topo)
+    twin = (col + 2) % len(cols)
+    return [at[(h, twin)], at[(near, col)], at[(near, twin)]]
+
+
+def _runs(ranks):
+    out = []
+    for i, r in enumerate(ranks):
+        if out and out[-1][1] + out[-1][2] == r * QP:
+            out[-1][2] += QP
+        else:
+            out.append([i * QP, r * QP, QP])
+    return out
+
+
+def rank_program(g, core, T, topo):
+    if T.rank_of(core) is None:
+        return
+    sem = T.sem
+    members = _group(core, T, topo)
+    mi = members.index(core)
+    peers = _peers(core, T, topo)
+    bank = [T.p0, T.p1, T.p2, T.p3]
+    own = T.kv[:, mi * KV:(mi + 1) * KV]
+    add, vmax = AluOpType.add, AluOpType.max
+    order = (1, 2, 3, 0)
+
+    g.sync.dma_start(T.kv[:, mi * KV:mi * KV + 128], T.k[:, :]).then_inc(sem.ld_kv, 16)
+    g.scalar.dma_start(T.kv[:, mi * KV + 128:(mi + 1) * KV], T.v[:, :]).then_inc(sem.ld_kv, 16)
+    g.sync.dma_start(T.bs[:, :], T.b[:, :]).then_inc(sem.ld_qb, 16)
+    g.scalar.dma_start(T.qs[:, :], T.q[:, :]).then_inc(sem.ld_qb, 16)
+
+    sent = 0
+    h = topo.host(core)
+    mates = sorted((m for m in members if m != core), key=lambda m: (topo.host(m) == h, topo.chip(m) == topo.chip(core)))
+    mk = topo.mask(core, core)
+    for m in mates:
+        mk &= topo.mask(core, m)
+    ids = [topo.addr(m, core) for m in mates]
+    g.wait_ge(sem.ld_kv, 32)
+    g.remote_dma_fused([RemoteDMATransfer(dst_ids=[DstId(rid=r, pnc=p) for r, p in ids], dma_engine_mask=mk,
+                                          remote_sem=sem["kv%d" % mi], srcs=[own], dsts=[own for _ in mates])],
+                       local_sem=sem.sent)
+    sent += bin(mk).count("1")
+    for k in (1, 2, 3):
+        d = peers[k - 1]
+        rid, pid = topo.addr(d, core)
+        m = topo.mask(core, d)
+        nruns = len(_runs([T.rank_of(x) for x in _group(d, T, topo)]))
+        g.wait_ge(sem["ob%d" % k], 1 + nruns)
+        g.remote_dma(out_ap=T.ib[:, (k - 1) * W:k * W], in_ap=T.ob[:, (k - 1) * W:k * W], remote_sem=sem["bi%d" % k],
+                     local_sem=sem.sent, pid=pid, routing_id=rid, dma_engine_mask=m)
+        sent += bin(m).count("1")
+    for k in (1, 2, 3):
+        d = peers[k - 1]
+        rid, pid = topo.addr(d, core)
+        m = topo.mask(core, d)
+        g.wait_ge(sem["vc%d" % k], 1)
+        g.remote_dma(out_ap=T.oi[:, (k - 1) * QP:k * QP], in_ap=T.og[:, (k - 1) * QP:k * QP], remote_sem=sem["oi%d" % k],
+                     local_sem=sem.sent, pid=pid, routing_id=rid, dma_engine_mask=m)
+        sent += bin(m).count("1")
+    g.wait_ge(sem.sent, sent)
+
+    pe = g.tensor
+    pe.wait_ge(sem.ld_kv, 32)
+    pe.wait_ge(sem.ld_qb, 32)
+    for j, m in enumerate(members):
+        if m != core:
+            pe.wait_ge(sem["kv%d" % j], bin(topo.mask(m, core)).count("1"))
+    for c in order:
+        if c:
+            pe.wait_ge(sem["bi%d" % c], bin(topo.mask(peers[c - 1], core)).count("1"))
+        q = T.ib[:, (c - 1) * W:(c - 1) * W + QP] if c else T.qs[:, :]
+        for j in range(G):
+            pe.matmul(bank[c][:, j * QP:(j + 1) * QP], T.kv[:, j * KV:j * KV + 128], q, True, True).then_inc(sem["ps%d" % c], 1)
+        pe.wait_ge(sem["vr%d" % c], 1)
+        for j in range(G):
+            pe.matmul(bank[c][:, 0:QP], T.kv[:, j * KV + 128:(j + 1) * KV], T.ss[:, (c * G + j) * QP:(c * G + j + 1) * QP],
+                      j == 0, j == G - 1).then_inc(sem["po%d" % c], 1)
+
+    ve = g.vector
+    ve.memset(T.zz[:, :], 0.0).then_inc(sem.zs, 1)
+    ve.wait_ge(sem.ld_qb, 32)
+    for k in (1, 2, 3):
+        o = (k - 1) * W
+        ve.tensor_copy(T.ob[:, o:o + QP], T.qs[:, :]).then_inc(sem["ob%d" % k], 1)
+        for dst, src, w in _runs([T.rank_of(x) for x in _group(peers[k - 1], T, topo)]):
+            ve.tensor_copy(T.ob[:, o + QP + dst:o + QP + dst + w], T.bs[:, src:src + w]).then_inc(sem["ob%d" % k], 1)
+    ve.wait_ge(sem.zs, 1)
+    SW = G * QP
+    for c in order:
+        ve.wait_ge(sem["ps%d" % c], G)
+        if c:
+            ve.wait_ge(sem["bi%d" % c], bin(topo.mask(peers[c - 1], core)).count("1"))
+            o = (c - 1) * W + QP
+            ve.tensor_tensor(bank[c][:, SW:2 * SW], bank[c][:, 0:SW], T.ib[:, o:o + SW], add).then_inc(sem["va%d" % c], 1)
+            n = 1
+        else:
+            runs = _runs([T.rank_of(x) for x in members])
+            for dst, src, w in runs:
+                ve.tensor_tensor(bank[c][:, SW + dst:SW + dst + w], bank[c][:, dst:dst + w], T.bs[:, src:src + w],
+                                 add).then_inc(sem["va%d" % c], 1)
+            n = len(runs)
+        ve.wait_ge(sem["va%d" % c], n)
+        ve.tensor_tensor(T.ss[:, c * SW:(c + 1) * SW], bank[c][:, SW:2 * SW], T.zz[:, :], vmax).then_inc(sem["vr%d" % c], 1)
+        if c:
+            ve.wait_ge(sem["po%d" % c], G)
+            ve.tensor_copy(T.og[:, (c - 1) * QP:c * QP], bank[c][:, 0:QP]).then_inc(sem["vc%d" % c], 1)
+    ne_in = [bin(topo.mask(p, core)).count("1") for p in peers]
+    ve.wait_ge(sem.po0, G)
+    ve.wait_ge(sem.oi1, ne_in[0])
+    ve.tensor_tensor(T.p0[:, QP:2 * QP], T.p0[:, 0:QP], T.oi[:, 0:QP], add).then_inc(sem.a1, 1)
+    ve.wait_ge(sem.a1, 1)
+    ve.wait_ge(sem.oi2, ne_in[1])
+    ve.tensor_tensor(T.p0[:, 2 * QP:3 * QP], T.p0[:, QP:2 * QP], T.oi[:, QP:2 * QP], add).then_inc(sem.a2, 1)
+    ve.wait_ge(sem.a2, 1)
+    ve.wait_ge(sem.oi3, ne_in[2])
+    ve.tensor_tensor(T.ys[:, :], T.p0[:, 2 * QP:3 * QP], T.oi[:, 2 * QP:3 * QP], add).then_inc(sem.vy, 1)
+
+    g.sync.wait_ge(sem.vy, 1)
+    g.sync.dma_start(T.y[:, :], T.ys[:, :]).then_inc(sem.st, 16)
+    g.sync.wait_ge(sem.st, 16)

@@ -22,7 +22,8 @@ SCRATCH = {
     "p2": ("psum", [128, 512], "float32"),
     "p3": ("psum", [128, 512], "float32"),
 }
-SEMAPHORES = (["ld_kv", "ld_qb", "zs", "sent", "vy", "st", "a1", "a2"]
+KV_SELF = 1
+SEMAPHORES = (["hk", "ld_kv", "ld_qb", "zs", "sent", "vy", "st", "a1", "a2"]
               + ["kv%d" % i for i in range(G)]
               + ["%s%d" % (n, i) for n in ("ps", "va", "vr", "po") for i in range(4)]
               + ["%s%d" % (n, i) for n in ("ob", "bi", "vc", "oi") for i in range(1, 4)])
@@ -67,8 +68,38 @@ def _runs(ranks):
     return out
 
 
+def _helper(core, T, topo):
+    same = [x for x in range(max(core - 8, 0), core + 8) if x != core and topo.host(x) == topo.host(core) and topo.chip(x) == topo.chip(core)]
+    return [x for x in same if T.rank_of(x) is None and topo.die(x) != topo.die(core)][0]
+
+
+def _kv_plan(core, T, topo):
+    members = _group(core, T, topo)
+    h = topo.host(core)
+    mates = sorted((m for m in members if m != core), key=lambda m: (topo.host(m) == h, topo.chip(m) == topo.chip(core)))
+    return members.index(core), mates[:KV_SELF], mates[KV_SELF:]
+
+
+def _send_kv(g, src, mi, dsts, T, topo, local_sem):
+    mk = topo.mask(src, src)
+    for m in dsts:
+        mk &= topo.mask(src, m)
+    ids = [topo.addr(m, src) for m in dsts]
+    own = T.kv[:, mi * KV:(mi + 1) * KV]
+    g.remote_dma_fused([RemoteDMATransfer(dst_ids=[DstId(rid=r, pnc=p) for r, p in ids], dma_engine_mask=mk,
+                                          remote_sem=T.sem["kv%d" % mi], srcs=[own], dsts=[own for _ in dsts])],
+                       local_sem=local_sem)
+    return bin(mk).count("1")
+
+
 def rank_program(g, core, T, topo):
     if T.rank_of(core) is None:
+        for c in T.cores:
+            mi, _, rest = _kv_plan(c, T, topo)
+            if rest and _helper(c, T, topo) == core:
+                g.wait_ge(T.sem.hk, bin(topo.mask(c, core) & ~topo.mask(c, rest[0])).count("1"))
+                n = _send_kv(g, core, mi, rest, T, topo, T.sem.sent)
+                g.wait_ge(T.sem.sent, n)
         return
     sem = T.sem
     members = _group(core, T, topo)
@@ -85,17 +116,16 @@ def rank_program(g, core, T, topo):
     g.scalar.dma_start(T.qs[:, :], T.q[:, :]).then_inc(sem.ld_qb, 16)
 
     sent = 0
-    h = topo.host(core)
-    mates = sorted((m for m in members if m != core), key=lambda m: (topo.host(m) == h, topo.chip(m) == topo.chip(core)))
-    mk = topo.mask(core, core)
-    for m in mates:
-        mk &= topo.mask(core, m)
-    ids = [topo.addr(m, core) for m in mates]
+    _, mine, rest = _kv_plan(core, T, topo)
     g.wait_ge(sem.ld_kv, 32)
-    g.remote_dma_fused([RemoteDMATransfer(dst_ids=[DstId(rid=r, pnc=p) for r, p in ids], dma_engine_mask=mk,
-                                          remote_sem=sem["kv%d" % mi], srcs=[own], dsts=[own for _ in mates])],
-                       local_sem=sem.sent)
-    sent += bin(mk).count("1")
+    if rest:
+        hp = _helper(core, T, topo)
+        rid, pid = topo.addr(hp, core)
+        m = topo.mask(core, hp) & ~topo.mask(core, rest[0])
+        g.remote_dma(out_ap=own, in_ap=own, remote_sem=sem.hk, local_sem=sem.sent, pid=pid, routing_id=rid, dma_engine_mask=m)
+        sent += bin(m).count("1")
+    if mine:
+        sent += _send_kv(g, core, mi, mine, T, topo, sem.sent)
     for k in (1, 2, 3):
         d = peers[k - 1]
         rid, pid = topo.addr(d, core)
@@ -118,14 +148,14 @@ def rank_program(g, core, T, topo):
     pe = g.tensor
     pe.wait_ge(sem.ld_kv, 32)
     pe.wait_ge(sem.ld_qb, 32)
-    for j, m in enumerate(members):
-        if m != core:
-            pe.wait_ge(sem["kv%d" % j], bin(topo.mask(m, core)).count("1"))
+    jord = sorted(range(G), key=lambda j: (members[j] != core, core not in _kv_plan(members[j], T, topo)[1]))
     for c in order:
         if c:
             pe.wait_ge(sem["bi%d" % c], bin(topo.mask(peers[c - 1], core)).count("1"))
         q = T.ib[:, (c - 1) * W:(c - 1) * W + QP] if c else T.qs[:, :]
-        for j in range(G):
+        for j in jord:
+            if c == order[0] and members[j] != core:
+                pe.wait_ge(sem["kv%d" % j], bin(topo.mask(members[j], core)).count("1"))
             pe.matmul(bank[c][:, j * QP:(j + 1) * QP], T.kv[:, j * KV:j * KV + 128], q, True, True).then_inc(sem["ps%d" % c], 1)
         pe.wait_ge(sem["vr%d" % c], 1)
         for j in range(G):

@@ -108,7 +108,7 @@ def rank_program(g, core, T, topo):
     bank = [T.p0, T.p1, T.p2, T.p3]
     own = T.kv[:, mi * KV:(mi + 1) * KV]
     add, vmax = AluOpType.add, AluOpType.max
-    order = (1, 2, 3, 0)
+    n_in = [0] + [bin(topo.mask(p, core)).count("1") for p in peers]
 
     g.sync.dma_start(T.kv[:, mi * KV:mi * KV + 128], T.k[:, :]).then_inc(sem.ld_kv, 16)
     g.scalar.dma_start(T.kv[:, mi * KV + 128:(mi + 1) * KV], T.v[:, :]).then_inc(sem.ld_kv, 16)
@@ -149,18 +149,30 @@ def rank_program(g, core, T, topo):
     pe.wait_ge(sem.ld_kv, 32)
     pe.wait_ge(sem.ld_qb, 32)
     jord = sorted(range(G), key=lambda j: (members[j] != core, core not in _kv_plan(members[j], T, topo)[1]))
-    for c in order:
+
+    def pe_s(c, first):
         if c:
-            pe.wait_ge(sem["bi%d" % c], bin(topo.mask(peers[c - 1], core)).count("1"))
+            pe.wait_ge(sem["bi%d" % c], n_in[c])
         q = T.ib[:, (c - 1) * W:(c - 1) * W + QP] if c else T.qs[:, :]
         for j in jord:
-            if c == order[0] and members[j] != core:
+            if first and members[j] != core:
                 pe.wait_ge(sem["kv%d" % j], bin(topo.mask(members[j], core)).count("1"))
             pe.matmul(bank[c][:, j * QP:(j + 1) * QP], T.kv[:, j * KV:j * KV + 128], q, True, True).then_inc(sem["ps%d" % c], 1)
+
+    def pe_o(c):
         pe.wait_ge(sem["vr%d" % c], 1)
         for j in range(G):
             pe.matmul(bank[c][:, 0:QP], T.kv[:, j * KV + 128:(j + 1) * KV], T.ss[:, (c * G + j) * QP:(c * G + j + 1) * QP],
                       j == 0, j == G - 1).then_inc(sem["po%d" % c], 1)
+
+    pe_s(1, True)
+    pe_s(2, False)
+    pe_o(1)
+    pe_s(3, False)
+    pe_o(2)
+    pe_o(3)
+    pe_s(0, False)
+    pe_o(0)
 
     ve = g.vector
     ve.memset(T.zz[:, :], 0.0).then_inc(sem.zs, 1)
@@ -172,10 +184,11 @@ def rank_program(g, core, T, topo):
             ve.tensor_copy(T.ob[:, o + QP + dst:o + QP + dst + w], T.bs[:, src:src + w]).then_inc(sem["ob%d" % k], 1)
     ve.wait_ge(sem.zs, 1)
     SW = G * QP
-    for c in order:
+
+    def ve_s(c):
         ve.wait_ge(sem["ps%d" % c], G)
         if c:
-            ve.wait_ge(sem["bi%d" % c], bin(topo.mask(peers[c - 1], core)).count("1"))
+            ve.wait_ge(sem["bi%d" % c], n_in[c])
             o = (c - 1) * W + QP
             ve.tensor_tensor(bank[c][:, SW:2 * SW], bank[c][:, 0:SW], T.ib[:, o:o + SW], add).then_inc(sem["va%d" % c], 1)
             n = 1
@@ -187,18 +200,26 @@ def rank_program(g, core, T, topo):
             n = len(runs)
         ve.wait_ge(sem["va%d" % c], n)
         ve.tensor_tensor(T.ss[:, c * SW:(c + 1) * SW], bank[c][:, SW:2 * SW], T.zz[:, :], vmax).then_inc(sem["vr%d" % c], 1)
-        if c:
-            ve.wait_ge(sem["po%d" % c], G)
-            ve.tensor_copy(T.og[:, (c - 1) * QP:c * QP], bank[c][:, 0:QP]).then_inc(sem["vc%d" % c], 1)
-    ne_in = [bin(topo.mask(p, core)).count("1") for p in peers]
+
+    def ve_o(c):
+        ve.wait_ge(sem["po%d" % c], G)
+        ve.tensor_copy(T.og[:, (c - 1) * QP:c * QP], bank[c][:, 0:QP]).then_inc(sem["vc%d" % c], 1)
+
+    ve_s(1)
+    ve_s(2)
+    ve_o(1)
+    ve_s(3)
+    ve_o(2)
+    ve_o(3)
+    ve_s(0)
     ve.wait_ge(sem.po0, G)
-    ve.wait_ge(sem.oi1, ne_in[0])
+    ve.wait_ge(sem.oi1, n_in[1])
     ve.tensor_tensor(T.p0[:, QP:2 * QP], T.p0[:, 0:QP], T.oi[:, 0:QP], add).then_inc(sem.a1, 1)
     ve.wait_ge(sem.a1, 1)
-    ve.wait_ge(sem.oi2, ne_in[1])
+    ve.wait_ge(sem.oi2, n_in[2])
     ve.tensor_tensor(T.p0[:, 2 * QP:3 * QP], T.p0[:, QP:2 * QP], T.oi[:, QP:2 * QP], add).then_inc(sem.a2, 1)
     ve.wait_ge(sem.a2, 1)
-    ve.wait_ge(sem.oi3, ne_in[2])
+    ve.wait_ge(sem.oi3, n_in[3])
     ve.tensor_tensor(T.ys[:, :], T.p0[:, 2 * QP:3 * QP], T.oi[:, 2 * QP:3 * QP], add).then_inc(sem.vy, 1)
 
     g.sync.wait_ge(sem.vy, 1)

@@ -12,21 +12,21 @@ SCRATCH = {
     "qs": ("sbuf", [128, QP], "bfloat16"),
     "ob": ("sbuf", [128, 3 * W], "bfloat16"),
     "ib": ("sbuf", [128, 3 * W], "bfloat16"),
-    "zz": ("sbuf", [128, G * QP], "bfloat16"),
+    "on": ("sbuf", [128, 128], "bfloat16"),
+    "idn": ("sbuf", [128, 128], "bfloat16"),
     "ss": ("sbuf", [128, 4 * G * QP], "bfloat16"),
     "og": ("sbuf", [128, 3 * QP], "bfloat16"),
     "oi": ("sbuf", [128, 3 * QP], "bfloat16"),
     "ys": ("sbuf", [128, QP], "bfloat16"),
-    "p0": ("psum", [128, 512], "float32"),
-    "p1": ("psum", [128, 512], "float32"),
-    "p2": ("psum", [128, 512], "float32"),
-    "p3": ("psum", [128, 512], "float32"),
 }
+for _c in range(4):
+    SCRATCH["p%d" % _c] = ("psum", [128, 512], "float32")
+    SCRATCH["r%d" % _c] = ("psum", [128, 512], "float32")
 KV_SELF = 1
-SEMAPHORES = (["hk", "ld_kv", "ld_qb", "zs", "sent", "vy", "st", "a1", "a2"]
+SEMAPHORES = (["hk", "ld_kv", "ld_qb", "o1", "idr", "sent", "vy", "st", "a1", "a2", "va0"]
               + ["kv%d" % i for i in range(G)]
-              + ["%s%d" % (n, i) for n in ("ps", "va", "vr", "po") for i in range(4)]
-              + ["%s%d" % (n, i) for n in ("ob", "bi", "vc", "oi") for i in range(1, 4)])
+              + ["%s%d" % (n, i) for n in ("ps", "vr", "po") for i in range(4)]
+              + ["%s%d" % (n, i) for n in ("ob", "bi", "pb", "vc", "oi") for i in range(1, 4)])
 
 
 def _layout(T, topo):
@@ -106,15 +106,19 @@ def rank_program(g, core, T, topo):
     mi = members.index(core)
     peers = _peers(core, T, topo)
     bank = [T.p0, T.p1, T.p2, T.p3]
+    obank = [T.r0, T.r1, T.r2, T.r3]
     own = T.kv[:, mi * KV:(mi + 1) * KV]
     add, vmax = AluOpType.add, AluOpType.max
     n_in = [0] + [bin(topo.mask(p, core)).count("1") for p in peers]
+    SW = G * QP
 
     g.sync.dma_start(T.kv[:, mi * KV:mi * KV + 128], T.k[:, :]).then_inc(sem.ld_kv, 16)
     g.scalar.dma_start(T.kv[:, mi * KV + 128:(mi + 1) * KV], T.v[:, :]).then_inc(sem.ld_kv, 16)
     g.sync.dma_start(T.bs[:, :], T.b[:, :]).then_inc(sem.ld_qb, 16)
     g.scalar.dma_start(T.qs[:, :], T.q[:, :]).then_inc(sem.ld_qb, 16)
 
+    g.wait_ge(sem.o1, 1)
+    g.affine_select(T.idn[:, :], T.on[:, :], [[-1, 128]], AluOpType.is_equal, 0.0, 0, 1).then_inc(sem.idr, 1)
     sent = 0
     _, mine, rest = _kv_plan(core, T, topo)
     g.wait_ge(sem.ld_kv, 32)
@@ -148,79 +152,86 @@ def rank_program(g, core, T, topo):
     pe = g.tensor
     pe.wait_ge(sem.ld_kv, 32)
     pe.wait_ge(sem.ld_qb, 32)
+    pe.wait_ge(sem.idr, 1)
     jord = sorted(range(G), key=lambda j: (members[j] != core, core not in _kv_plan(members[j], T, topo)[1]))
+    seen = set()
 
-    def pe_s(c, first):
+    def pe_b(c):
+        pe.wait_ge(sem["bi%d" % c], n_in[c])
+        o = (c - 1) * W + QP
+        pe.matmul(bank[c][:, 0:SW], T.idn[:, :], T.ib[:, o:o + SW], True, False).then_inc(sem["pb%d" % c], 1)
+
+    def pe_s(c):
         if c:
-            pe.wait_ge(sem["bi%d" % c], n_in[c])
+            pe.wait_ge(sem["pb%d" % c], 1)
         q = T.ib[:, (c - 1) * W:(c - 1) * W + QP] if c else T.qs[:, :]
-        for j in jord:
-            if first and members[j] != core:
+        for i, j in enumerate(jord):
+            if j not in seen and members[j] != core:
                 pe.wait_ge(sem["kv%d" % j], bin(topo.mask(members[j], core)).count("1"))
-            pe.matmul(bank[c][:, j * QP:(j + 1) * QP], T.kv[:, j * KV:j * KV + 128], q, True, True).then_inc(sem["ps%d" % c], 1)
+            seen.add(j)
+            pe.matmul(bank[c][:, j * QP:(j + 1) * QP], T.kv[:, j * KV:j * KV + 128], q, c == 0,
+                      c == 0 or i == G - 1).then_inc(sem["ps%d" % c], 1)
 
     def pe_o(c):
         pe.wait_ge(sem["vr%d" % c], 1)
         for j in range(G):
-            pe.matmul(bank[c][:, 0:QP], T.kv[:, j * KV + 128:(j + 1) * KV], T.ss[:, (c * G + j) * QP:(c * G + j + 1) * QP],
+            pe.matmul(obank[c][:, 0:QP], T.kv[:, j * KV + 128:(j + 1) * KV], T.ss[:, (c * G + j) * QP:(c * G + j + 1) * QP],
                       j == 0, j == G - 1).then_inc(sem["po%d" % c], 1)
 
-    pe_s(1, True)
-    pe_s(2, False)
+    pe_b(1)
+    pe_b(2)
+    pe_s(1)
+    pe_s(2)
+    pe_b(3)
+    pe_s(3)
     pe_o(1)
-    pe_s(3, False)
     pe_o(2)
     pe_o(3)
-    pe_s(0, False)
+    pe_s(0)
     pe_o(0)
 
     ve = g.vector
-    ve.memset(T.zz[:, :], 0.0).then_inc(sem.zs, 1)
+    ve.memset(T.on[:, :], 1.0).then_inc(sem.o1, 1)
     ve.wait_ge(sem.ld_qb, 32)
     for k in (1, 2, 3):
         o = (k - 1) * W
         ve.tensor_copy(T.ob[:, o:o + QP], T.qs[:, :]).then_inc(sem["ob%d" % k], 1)
         for dst, src, w in _runs([T.rank_of(x) for x in _group(peers[k - 1], T, topo)]):
             ve.tensor_copy(T.ob[:, o + QP + dst:o + QP + dst + w], T.bs[:, src:src + w]).then_inc(sem["ob%d" % k], 1)
-    ve.wait_ge(sem.zs, 1)
-    SW = G * QP
 
     def ve_s(c):
         ve.wait_ge(sem["ps%d" % c], G)
-        if c:
-            ve.wait_ge(sem["bi%d" % c], n_in[c])
-            o = (c - 1) * W + QP
-            ve.tensor_tensor(bank[c][:, SW:2 * SW], bank[c][:, 0:SW], T.ib[:, o:o + SW], add).then_inc(sem["va%d" % c], 1)
-            n = 1
-        else:
+        lo = 0
+        if c == 0:
             runs = _runs([T.rank_of(x) for x in members])
             for dst, src, w in runs:
                 ve.tensor_tensor(bank[c][:, SW + dst:SW + dst + w], bank[c][:, dst:dst + w], T.bs[:, src:src + w],
-                                 add).then_inc(sem["va%d" % c], 1)
-            n = len(runs)
-        ve.wait_ge(sem["va%d" % c], n)
-        ve.tensor_tensor(T.ss[:, c * SW:(c + 1) * SW], bank[c][:, SW:2 * SW], T.zz[:, :], vmax).then_inc(sem["vr%d" % c], 1)
+                                 add).then_inc(sem.va0, 1)
+            ve.wait_ge(sem.va0, len(runs))
+            lo = SW
+        ve.tensor_scalar(T.ss[:, c * SW:(c + 1) * SW], bank[c][:, lo:lo + SW], 0.0, None, vmax).then_inc(sem["vr%d" % c], 1)
 
     def ve_o(c):
         ve.wait_ge(sem["po%d" % c], G)
-        ve.tensor_copy(T.og[:, (c - 1) * QP:c * QP], bank[c][:, 0:QP]).then_inc(sem["vc%d" % c], 1)
+        ve.tensor_copy(T.og[:, (c - 1) * QP:c * QP], obank[c][:, 0:QP]).then_inc(sem["vc%d" % c], 1)
 
     ve_s(1)
     ve_s(2)
-    ve_o(1)
     ve_s(3)
+    ve_o(1)
     ve_o(2)
     ve_o(3)
     ve_s(0)
+    p = obank[0]
     ve.wait_ge(sem.po0, G)
     ve.wait_ge(sem.oi1, n_in[1])
-    ve.tensor_tensor(T.p0[:, QP:2 * QP], T.p0[:, 0:QP], T.oi[:, 0:QP], add).then_inc(sem.a1, 1)
+    ve.tensor_tensor(p[:, QP:2 * QP], p[:, 0:QP], T.oi[:, 0:QP], add).then_inc(sem.a1, 1)
     ve.wait_ge(sem.a1, 1)
     ve.wait_ge(sem.oi2, n_in[2])
-    ve.tensor_tensor(T.p0[:, 2 * QP:3 * QP], T.p0[:, QP:2 * QP], T.oi[:, QP:2 * QP], add).then_inc(sem.a2, 1)
+    ve.tensor_tensor(p[:, 2 * QP:3 * QP], p[:, QP:2 * QP], T.oi[:, QP:2 * QP], add).then_inc(sem.a2, 1)
     ve.wait_ge(sem.a2, 1)
     ve.wait_ge(sem.oi3, n_in[3])
-    ve.tensor_tensor(T.ys[:, :], T.p0[:, 2 * QP:3 * QP], T.oi[:, 2 * QP:3 * QP], add).then_inc(sem.vy, 1)
+    ve.tensor_tensor(T.ys[:, :], p[:, 2 * QP:3 * QP], T.oi[:, 2 * QP:3 * QP], add).then_inc(sem.vy, 1)
 
     g.sync.wait_ge(sem.vy, 1)
     g.sync.dma_start(T.y[:, :], T.ys[:, :]).then_inc(sem.st, 16)

@@ -5,14 +5,17 @@ QP = 64
 KV = 256
 G = 4
 W = QP * (1 + G)
+HALF = 64
+PIECE = 32
 
 SCRATCH = {
     "kv": ("sbuf", [128, G * KV], "bfloat16"),
     "bs": ("sbuf", [128, 16 * QP], "bfloat16"),
     "qs": ("sbuf", [128, QP], "bfloat16"),
+    "b0": ("sbuf", [128, G * QP], "bfloat16"),
     "ob": ("sbuf", [128, 3 * W], "bfloat16"),
     "ib": ("sbuf", [128, 3 * W], "bfloat16"),
-    "on": ("sbuf", [128, 128], "bfloat16"),
+    "on": ("sbuf", [128, HALF], "bfloat16"),
     "idn": ("sbuf", [128, 128], "bfloat16"),
     "ss": ("sbuf", [128, 4 * G * QP], "bfloat16"),
     "og": ("sbuf", [128, 3 * QP], "bfloat16"),
@@ -23,10 +26,14 @@ for _c in range(4):
     SCRATCH["p%d" % _c] = ("psum", [128, 512], "float32")
     SCRATCH["r%d" % _c] = ("psum", [128, 512], "float32")
 KV_SELF = 1
-SEMAPHORES = (["hk", "ld_kv", "ld_qb", "o1", "idr", "sent", "vy", "st", "a1", "a2", "va0"]
+SEMAPHORES = (["hk", "ld_kv", "ld_qb", "o1", "idl", "idr", "sent", "vy", "st", "a1", "a2"]
               + ["kv%d" % i for i in range(G)]
-              + ["%s%d" % (n, i) for n in ("ps", "vr", "po") for i in range(4)]
-              + ["%s%d" % (n, i) for n in ("ob", "bi", "pb", "vc", "oi") for i in range(1, 4)])
+              + ["%s%d" % (n, i) for n in ("ps", "vr", "po", "ob", "pb") for i in range(4)]
+              + ["%s%d" % (n, i) for n in ("bi", "vc", "oi") for i in range(1, 4)])
+
+
+def _bits(m):
+    return bin(m).count("1")
 
 
 def _layout(T, topo):
@@ -80,6 +87,10 @@ def _kv_plan(core, T, topo):
     return members.index(core), mates[:KV_SELF], mates[KV_SELF:]
 
 
+def _chip_only(core, hp, away, topo):
+    return topo.mask(core, hp) & ~topo.mask(core, away)
+
+
 def _send_kv(g, src, mi, dsts, T, topo, local_sem):
     mk = topo.mask(src, src)
     for m in dsts:
@@ -89,27 +100,42 @@ def _send_kv(g, src, mi, dsts, T, topo, local_sem):
     g.remote_dma_fused([RemoteDMATransfer(dst_ids=[DstId(rid=r, pnc=p) for r, p in ids], dma_engine_mask=mk,
                                           remote_sem=T.sem["kv%d" % mi], srcs=[own], dsts=[own for _ in dsts])],
                        local_sem=local_sem)
-    return bin(mk).count("1")
+    return _bits(mk)
+
+
+def _helper_program(g, core, c, T, topo):
+    sem = T.sem
+    mi, _, rest = _kv_plan(c, T, topo)
+    mk = topo.mask(core, c) & topo.mask(core, rest[0])
+    half = T.idn[:, HALF:2 * HALF]
+    g.vector.memset(T.on[:, :], 1.0).then_inc(sem.o1, 1)
+    g.wait_ge(sem.o1, 1)
+    g.affine_select(half, T.on[:, :], [[-1, HALF]], AluOpType.is_equal, 0.0, -HALF, 1).then_inc(sem.idl, 1)
+    g.wait_ge(sem.idl, 1)
+    rid, pid = topo.addr(c, core)
+    g.remote_dma(out_ap=half, in_ap=half, remote_sem=sem.idr, local_sem=sem.sent, pid=pid, routing_id=rid, dma_engine_mask=mk)
+    sent = _bits(mk)
+    g.wait_ge(sem.hk, _bits(_chip_only(c, core, rest[0], topo)))
+    sent += _send_kv(g, core, mi, rest, T, topo, sem.sent)
+    g.wait_ge(sem.sent, sent)
 
 
 def rank_program(g, core, T, topo):
     if T.rank_of(core) is None:
         for c in T.cores:
-            mi, _, rest = _kv_plan(c, T, topo)
-            if rest and _helper(c, T, topo) == core:
-                g.wait_ge(T.sem.hk, bin(topo.mask(c, core) & ~topo.mask(c, rest[0])).count("1"))
-                n = _send_kv(g, core, mi, rest, T, topo, T.sem.sent)
-                g.wait_ge(T.sem.sent, n)
+            if topo.host(c) == topo.host(core) and topo.chip(c) == topo.chip(core) and _helper(c, T, topo) == core:
+                _helper_program(g, core, c, T, topo)
         return
     sem = T.sem
     members = _group(core, T, topo)
     mi = members.index(core)
     peers = _peers(core, T, topo)
+    hp = _helper(core, T, topo)
     bank = [T.p0, T.p1, T.p2, T.p3]
     obank = [T.r0, T.r1, T.r2, T.r3]
     own = T.kv[:, mi * KV:(mi + 1) * KV]
     add, vmax = AluOpType.add, AluOpType.max
-    n_in = [0] + [bin(topo.mask(p, core)).count("1") for p in peers]
+    n_in = [0] + [_bits(topo.mask(p, core)) for p in peers]
     SW = G * QP
 
     g.sync.dma_start(T.kv[:, mi * KV:mi * KV + 128], T.k[:, :]).then_inc(sem.ld_kv, 16)
@@ -117,28 +143,31 @@ def rank_program(g, core, T, topo):
     g.sync.dma_start(T.bs[:, :], T.b[:, :]).then_inc(sem.ld_qb, 16)
     g.scalar.dma_start(T.qs[:, :], T.q[:, :]).then_inc(sem.ld_qb, 16)
 
-    g.wait_ge(sem.o1, 1)
-    g.affine_select(T.idn[:, :], T.on[:, :], [[-1, 128]], AluOpType.is_equal, 0.0, 0, 1).then_inc(sem.idr, 1)
     sent = 0
+    lo = PIECE if T.rank_of(core) > T.rank_of(peers[0]) else 0
+    piece = T.idn[:, lo:lo + PIECE]
+    g.wait_ge(sem.o1, 1)
+    g.affine_select(piece, T.on[:, 0:PIECE], [[-1, PIECE]], AluOpType.is_equal, 0.0, -lo, 1).then_inc(sem.idl, 1)
+    g.wait_ge(sem.idl, 1)
+    rid, pid = topo.addr(peers[0], core)
+    m = topo.mask(core, peers[0])
+    g.remote_dma(out_ap=piece, in_ap=piece, remote_sem=sem.idr, local_sem=sem.sent, pid=pid, routing_id=rid, dma_engine_mask=m)
+    sent += _bits(m)
     _, mine, rest = _kv_plan(core, T, topo)
     g.wait_ge(sem.ld_kv, 32)
-    if rest:
-        hp = _helper(core, T, topo)
-        rid, pid = topo.addr(hp, core)
-        m = topo.mask(core, hp) & ~topo.mask(core, rest[0])
-        g.remote_dma(out_ap=own, in_ap=own, remote_sem=sem.hk, local_sem=sem.sent, pid=pid, routing_id=rid, dma_engine_mask=m)
-        sent += bin(m).count("1")
-    if mine:
-        sent += _send_kv(g, core, mi, mine, T, topo, sem.sent)
+    rid, pid = topo.addr(hp, core)
+    m = _chip_only(core, hp, rest[0], topo)
+    g.remote_dma(out_ap=own, in_ap=own, remote_sem=sem.hk, local_sem=sem.sent, pid=pid, routing_id=rid, dma_engine_mask=m)
+    sent += _bits(m)
+    sent += _send_kv(g, core, mi, mine, T, topo, sem.sent)
     for k in (1, 2, 3):
-        d = peers[k - 1]
-        rid, pid = topo.addr(d, core)
-        m = topo.mask(core, d)
-        nruns = len(_runs([T.rank_of(x) for x in _group(d, T, topo)]))
+        nruns = len(_runs([T.rank_of(x) for x in _group(peers[k - 1], T, topo)]))
         g.wait_ge(sem["ob%d" % k], 1 + nruns)
+        rid, pid = topo.addr(peers[k - 1], core)
+        m = topo.mask(core, peers[k - 1])
         g.remote_dma(out_ap=T.ib[:, (k - 1) * W:k * W], in_ap=T.ob[:, (k - 1) * W:k * W], remote_sem=sem["bi%d" % k],
                      local_sem=sem.sent, pid=pid, routing_id=rid, dma_engine_mask=m)
-        sent += bin(m).count("1")
+        sent += _bits(m)
     for k in (1, 2, 3):
         d = peers[k - 1]
         rid, pid = topo.addr(d, core)
@@ -146,31 +175,37 @@ def rank_program(g, core, T, topo):
         g.wait_ge(sem["vc%d" % k], 1)
         g.remote_dma(out_ap=T.oi[:, (k - 1) * QP:k * QP], in_ap=T.og[:, (k - 1) * QP:k * QP], remote_sem=sem["oi%d" % k],
                      local_sem=sem.sent, pid=pid, routing_id=rid, dma_engine_mask=m)
-        sent += bin(m).count("1")
+        sent += _bits(m)
     g.wait_ge(sem.sent, sent)
 
     pe = g.tensor
-    pe.wait_ge(sem.ld_kv, 32)
-    pe.wait_ge(sem.ld_qb, 32)
-    pe.wait_ge(sem.idr, 1)
-    jord = sorted(range(G), key=lambda j: (members[j] != core, core not in _kv_plan(members[j], T, topo)[1]))
-    seen = set()
+    own_runs = _runs([T.rank_of(x) for x in members])
+    early = sorted((j for j in range(G) if members[j] == core or core in _kv_plan(members[j], T, topo)[1]),
+                   key=lambda j: members[j] != core)
+    late = [j for j in range(G) if j not in early]
+    seen, opened, done = set(), set(), {c: 0 for c in range(4)}
 
     def pe_b(c):
-        pe.wait_ge(sem["bi%d" % c], n_in[c])
-        o = (c - 1) * W + QP
-        pe.matmul(bank[c][:, 0:SW], T.idn[:, :], T.ib[:, o:o + SW], True, False).then_inc(sem["pb%d" % c], 1)
-
-    def pe_s(c):
         if c:
+            pe.wait_ge(sem["bi%d" % c], n_in[c])
+            o = (c - 1) * W + QP
+            tables = T.ib[:, o:o + SW]
+        else:
+            pe.wait_ge(sem.ob0, len(own_runs))
+            tables = T.b0[:, :]
+        pe.matmul(bank[c][:, 0:SW], T.idn[:, :], tables, True, False).then_inc(sem["pb%d" % c], 1)
+
+    def pe_s(c, j):
+        if j not in seen and members[j] != core:
+            pe.wait_ge(sem["kv%d" % j], _bits(topo.mask(members[j], core)))
+        seen.add(j)
+        if c not in opened:
             pe.wait_ge(sem["pb%d" % c], 1)
+        opened.add(c)
+        done[c] += 1
         q = T.ib[:, (c - 1) * W:(c - 1) * W + QP] if c else T.qs[:, :]
-        for i, j in enumerate(jord):
-            if j not in seen and members[j] != core:
-                pe.wait_ge(sem["kv%d" % j], bin(topo.mask(members[j], core)).count("1"))
-            seen.add(j)
-            pe.matmul(bank[c][:, j * QP:(j + 1) * QP], T.kv[:, j * KV:j * KV + 128], q, c == 0,
-                      c == 0 or i == G - 1).then_inc(sem["ps%d" % c], 1)
+        pe.matmul(bank[c][:, j * QP:(j + 1) * QP], T.kv[:, j * KV:j * KV + 128], q, False,
+                  done[c] == G).then_inc(sem["ps%d" % c], 1)
 
     def pe_o(c):
         pe.wait_ge(sem["vr%d" % c], 1)
@@ -178,38 +213,43 @@ def rank_program(g, core, T, topo):
             pe.matmul(obank[c][:, 0:QP], T.kv[:, j * KV + 128:(j + 1) * KV], T.ss[:, (c * G + j) * QP:(c * G + j + 1) * QP],
                       j == 0, j == G - 1).then_inc(sem["po%d" % c], 1)
 
+    pe.wait_ge(sem.ld_kv, 32)
+    pe.wait_ge(sem.ld_qb, 32)
+    pe.wait_ge(sem.idl, 1)
+    pe.wait_ge(sem.idr, n_in[1] + _bits(topo.mask(hp, core) & topo.mask(hp, rest[0])))
+    pe_b(0)
     pe_b(1)
     pe_b(2)
-    pe_s(1)
-    pe_s(2)
+    for j in early:
+        for c in (0, 1, 2):
+            pe_s(c, j)
+    for j in late:
+        for c in (1, 2):
+            pe_s(c, j)
     pe_b(3)
-    pe_s(3)
+    for j in early + late:
+        pe_s(3, j)
     pe_o(1)
     pe_o(2)
     pe_o(3)
-    pe_s(0)
+    for j in late:
+        pe_s(0, j)
     pe_o(0)
 
     ve = g.vector
-    ve.memset(T.on[:, :], 1.0).then_inc(sem.o1, 1)
+    ve.memset(T.on[:, 0:PIECE], 1.0).then_inc(sem.o1, 1)
     ve.wait_ge(sem.ld_qb, 32)
     for k in (1, 2, 3):
         o = (k - 1) * W
         ve.tensor_copy(T.ob[:, o:o + QP], T.qs[:, :]).then_inc(sem["ob%d" % k], 1)
         for dst, src, w in _runs([T.rank_of(x) for x in _group(peers[k - 1], T, topo)]):
             ve.tensor_copy(T.ob[:, o + QP + dst:o + QP + dst + w], T.bs[:, src:src + w]).then_inc(sem["ob%d" % k], 1)
+    for dst, src, w in own_runs:
+        ve.tensor_copy(T.b0[:, dst:dst + w], T.bs[:, src:src + w]).then_inc(sem.ob0, 1)
 
     def ve_s(c):
         ve.wait_ge(sem["ps%d" % c], G)
-        lo = 0
-        if c == 0:
-            runs = _runs([T.rank_of(x) for x in members])
-            for dst, src, w in runs:
-                ve.tensor_tensor(bank[c][:, SW + dst:SW + dst + w], bank[c][:, dst:dst + w], T.bs[:, src:src + w],
-                                 add).then_inc(sem.va0, 1)
-            ve.wait_ge(sem.va0, len(runs))
-            lo = SW
-        ve.tensor_scalar(T.ss[:, c * SW:(c + 1) * SW], bank[c][:, lo:lo + SW], 0.0, None, vmax).then_inc(sem["vr%d" % c], 1)
+        ve.tensor_scalar(T.ss[:, c * SW:(c + 1) * SW], bank[c][:, 0:SW], 0.0, None, vmax).then_inc(sem["vr%d" % c], 1)
 
     def ve_o(c):
         ve.wait_ge(sem["po%d" % c], G)

from concourse.bass import DstId, RemoteDMATransfer
from concourse.mybir import AluOpType

QP = 64
KV = 256
G = 4
W = QP * (1 + G)
HALF = 64
PIECE = 32

SCRATCH = {
    "kv": ("sbuf", [128, G * KV], "bfloat16"),
    "bs": ("sbuf", [128, 16 * QP], "bfloat16"),
    "qs": ("sbuf", [128, QP], "bfloat16"),
    "b0": ("sbuf", [128, G * QP], "bfloat16"),
    "ob": ("sbuf", [128, 3 * W], "bfloat16"),
    "ib": ("sbuf", [128, 3 * W], "bfloat16"),
    "on": ("sbuf", [128, HALF], "bfloat16"),
    "idn": ("sbuf", [128, 128], "bfloat16"),
    "ss": ("sbuf", [128, 4 * G * QP], "bfloat16"),
    "og": ("sbuf", [128, 3 * QP], "bfloat16"),
    "oi": ("sbuf", [128, 3 * QP], "bfloat16"),
    "ys": ("sbuf", [128, QP], "bfloat16"),
}
for _c in range(4):
    SCRATCH["p%d" % _c] = ("psum", [128, 512], "float32")
    SCRATCH["r%d" % _c] = ("psum", [128, 512], "float32")
KV_SELF = 1
SEMAPHORES = (["hk", "ld_kv", "ld_qb", "o1", "idl", "idr", "sent", "vy", "st", "a1", "a2"]
              + ["kv%d" % i for i in range(G)]
              + ["%s%d" % (n, i) for n in ("ps", "vr", "po", "ob", "pb") for i in range(4)]
              + ["%s%d" % (n, i) for n in ("bi", "vc", "oi") for i in range(1, 4)])


def _bits(m):
    return bin(m).count("1")


def _layout(T, topo):
    cols = sorted({topo.chip(c) for c in T.cores})
    at = {(topo.host(c), cols.index(topo.chip(c))): c for c in T.cores}
    return cols, at


def _place(core, T, topo):
    cols, at = _layout(T, topo)
    h, col = topo.host(core), cols.index(topo.chip(core))
    others = sorted({topo.host(c) for c in T.cores} - {h})
    near = [x for x in others if topo.rack(x) == topo.rack(h)][0]
    far = [x for x in others if topo.rack(x) != topo.rack(h) and topo.may_write(core, at[(x, col)])][0]
    return h, col, near, far


def _group(core, T, topo):
    _, at = _layout(T, topo)
    h, col, _, far = _place(core, T, topo)
    first = col - col % 2
    return sorted((at[(x, c)] for x in (h, far) for c in (first, first + 1)), key=T.rank_of)


def _peers(core, T, topo):
    cols, at = _layout(T, topo)
    h, col, near, _ = _place(core, T, topo)
    twin = (col + 2) % len(cols)
    return [at[(h, twin)], at[(near, col)], at[(near, twin)]]


def _runs(ranks):
    out = []
    for i, r in enumerate(ranks):
        if out and out[-1][1] + out[-1][2] == r * QP:
            out[-1][2] += QP
        else:
            out.append([i * QP, r * QP, QP])
    return out


def _helper(core, T, topo):
    same = [x for x in range(max(core - 8, 0), core + 8) if x != core and topo.host(x) == topo.host(core) and topo.chip(x) == topo.chip(core)]
    return [x for x in same if T.rank_of(x) is None and topo.die(x) != topo.die(core)][0]


def _kv_plan(core, T, topo):
    members = _group(core, T, topo)
    h = topo.host(core)
    mates = sorted((m for m in members if m != core), key=lambda m: (topo.host(m) == h, topo.chip(m) == topo.chip(core)))
    return members.index(core), mates[:KV_SELF], mates[KV_SELF:]


def _chip_only(core, hp, away, topo):
    return topo.mask(core, hp) & ~topo.mask(core, away)


def _send_kv(g, src, mi, dsts, T, topo, local_sem):
    mk = topo.mask(src, src)
    for m in dsts:
        mk &= topo.mask(src, m)
    ids = [topo.addr(m, src) for m in dsts]
    own = T.kv[:, mi * KV:(mi + 1) * KV]
    g.remote_dma_fused([RemoteDMATransfer(dst_ids=[DstId(rid=r, pnc=p) for r, p in ids], dma_engine_mask=mk,
                                          remote_sem=T.sem["kv%d" % mi], srcs=[own], dsts=[own for _ in dsts])],
                       local_sem=local_sem)
    return _bits(mk)


def _helper_program(g, core, c, T, topo):
    sem = T.sem
    mi, _, rest = _kv_plan(c, T, topo)
    mk = topo.mask(core, c) & topo.mask(core, rest[0])
    half = T.idn[:, HALF:2 * HALF]
    g.vector.memset(T.on[:, :], 1.0).then_inc(sem.o1, 1)
    g.wait_ge(sem.o1, 1)
    g.affine_select(half, T.on[:, :], [[-1, HALF]], AluOpType.is_equal, 0.0, -HALF, 1).then_inc(sem.idl, 1)
    g.wait_ge(sem.idl, 1)
    rid, pid = topo.addr(c, core)
    g.remote_dma(out_ap=half, in_ap=half, remote_sem=sem.idr, local_sem=sem.sent, pid=pid, routing_id=rid, dma_engine_mask=mk)
    sent = _bits(mk)
    g.wait_ge(sem.hk, _bits(_chip_only(c, core, rest[0], topo)))
    sent += _send_kv(g, core, mi, rest, T, topo, sem.sent)
    g.wait_ge(sem.sent, sent)


def rank_program(g, core, T, topo):
    if T.rank_of(core) is None:
        for c in T.cores:
            if topo.host(c) == topo.host(core) and topo.chip(c) == topo.chip(core) and _helper(c, T, topo) == core:
                _helper_program(g, core, c, T, topo)
        return
    sem = T.sem
    members = _group(core, T, topo)
    mi = members.index(core)
    peers = _peers(core, T, topo)
    hp = _helper(core, T, topo)
    bank = [T.p0, T.p1, T.p2, T.p3]
    obank = [T.r0, T.r1, T.r2, T.r3]
    own = T.kv[:, mi * KV:(mi + 1) * KV]
    add, vmax = AluOpType.add, AluOpType.max
    n_in = [0] + [_bits(topo.mask(p, core)) for p in peers]
    SW = G * QP

    g.sync.dma_start(T.kv[:, mi * KV:mi * KV + 128], T.k[:, :]).then_inc(sem.ld_kv, 16)
    g.scalar.dma_start(T.kv[:, mi * KV + 128:(mi + 1) * KV], T.v[:, :]).then_inc(sem.ld_kv, 16)
    g.sync.dma_start(T.bs[:, :], T.b[:, :]).then_inc(sem.ld_qb, 16)
    g.scalar.dma_start(T.qs[:, :], T.q[:, :]).then_inc(sem.ld_qb, 16)

    sent = 0
    lo = PIECE if T.rank_of(core) > T.rank_of(peers[0]) else 0
    piece = T.idn[:, lo:lo + PIECE]
    g.wait_ge(sem.o1, 1)
    g.affine_select(piece, T.on[:, 0:PIECE], [[-1, PIECE]], AluOpType.is_equal, 0.0, -lo, 1).then_inc(sem.idl, 1)
    g.wait_ge(sem.idl, 1)
    rid, pid = topo.addr(peers[0], core)
    m = topo.mask(core, peers[0])
    g.remote_dma(out_ap=piece, in_ap=piece, remote_sem=sem.idr, local_sem=sem.sent, pid=pid, routing_id=rid, dma_engine_mask=m)
    sent += _bits(m)
    _, mine, rest = _kv_plan(core, T, topo)
    g.wait_ge(sem.ld_kv, 32)
    rid, pid = topo.addr(hp, core)
    m = _chip_only(core, hp, rest[0], topo)
    g.remote_dma(out_ap=own, in_ap=own, remote_sem=sem.hk, local_sem=sem.sent, pid=pid, routing_id=rid, dma_engine_mask=m)
    sent += _bits(m)
    sent += _send_kv(g, core, mi, mine, T, topo, sem.sent)
    for k in (1, 2, 3):
        nruns = len(_runs([T.rank_of(x) for x in _group(peers[k - 1], T, topo)]))
        g.wait_ge(sem["ob%d" % k], 1 + nruns)
        rid, pid = topo.addr(peers[k - 1], core)
        m = topo.mask(core, peers[k - 1])
        g.remote_dma(out_ap=T.ib[:, (k - 1) * W:k * W], in_ap=T.ob[:, (k - 1) * W:k * W], remote_sem=sem["bi%d" % k],
                     local_sem=sem.sent, pid=pid, routing_id=rid, dma_engine_mask=m)
        sent += _bits(m)
    for k in (1, 2, 3):
        d = peers[k - 1]
        rid, pid = topo.addr(d, core)
        m = topo.mask(core, d)
        g.wait_ge(sem["vc%d" % k], 1)
        g.remote_dma(out_ap=T.oi[:, (k - 1) * QP:k * QP], in_ap=T.og[:, (k - 1) * QP:k * QP], remote_sem=sem["oi%d" % k],
                     local_sem=sem.sent, pid=pid, routing_id=rid, dma_engine_mask=m)
        sent += _bits(m)
    g.wait_ge(sem.sent, sent)

    pe = g.tensor
    own_runs = _runs([T.rank_of(x) for x in members])
    early = sorted((j for j in range(G) if members[j] == core or core in _kv_plan(members[j], T, topo)[1]),
                   key=lambda j: members[j] != core)
    late = [j for j in range(G) if j not in early]
    seen, opened, done = set(), set(), {c: 0 for c in range(4)}

    def pe_b(c):
        if c:
            pe.wait_ge(sem["bi%d" % c], n_in[c])
            o = (c - 1) * W + QP
            tables = T.ib[:, o:o + SW]
        else:
            pe.wait_ge(sem.ob0, len(own_runs))
            tables = T.b0[:, :]
        pe.matmul(bank[c][:, 0:SW], T.idn[:, :], tables, True, False).then_inc(sem["pb%d" % c], 1)

    def pe_s(c, j):
        if j not in seen and members[j] != core:
            pe.wait_ge(sem["kv%d" % j], _bits(topo.mask(members[j], core)))
        seen.add(j)
        if c not in opened:
            pe.wait_ge(sem["pb%d" % c], 1)
        opened.add(c)
        done[c] += 1
        q = T.ib[:, (c - 1) * W:(c - 1) * W + QP] if c else T.qs[:, :]
        pe.matmul(bank[c][:, j * QP:(j + 1) * QP], T.kv[:, j * KV:j * KV + 128], q, False,
                  done[c] == G).then_inc(sem["ps%d" % c], 1)

    def pe_o(c):
        pe.wait_ge(sem["vr%d" % c], 1)
        for j in range(G):
            pe.matmul(obank[c][:, 0:QP], T.kv[:, j * KV + 128:(j + 1) * KV], T.ss[:, (c * G + j) * QP:(c * G + j + 1) * QP],
                      j == 0, j == G - 1).then_inc(sem["po%d" % c], 1)

    pe.wait_ge(sem.ld_kv, 32)
    pe.wait_ge(sem.ld_qb, 32)
    pe.wait_ge(sem.idl, 1)
    pe.wait_ge(sem.idr, n_in[1] + _bits(topo.mask(hp, core) & topo.mask(hp, rest[0])))
    pe_b(0)
    pe_b(1)
    pe_b(2)
    for j in early:
        for c in (0, 1, 2):
            pe_s(c, j)
    for j in late:
        for c in (1, 2):
            pe_s(c, j)
    pe_b(3)
    for j in early + late:
        pe_s(3, j)
    pe_o(1)
    pe_o(2)
    pe_o(3)
    for j in late:
        pe_s(0, j)
    pe_o(0)

    ve = g.vector
    ve.memset(T.on[:, 0:PIECE], 1.0).then_inc(sem.o1, 1)
    ve.wait_ge(sem.ld_qb, 32)
    for k in (1, 2, 3):
        o = (k - 1) * W
        ve.tensor_copy(T.ob[:, o:o + QP], T.qs[:, :]).then_inc(sem["ob%d" % k], 1)
        for dst, src, w in _runs([T.rank_of(x) for x in _group(peers[k - 1], T, topo)]):
            ve.tensor_copy(T.ob[:, o + QP + dst:o + QP + dst + w], T.bs[:, src:src + w]).then_inc(sem["ob%d" % k], 1)
    for dst, src, w in own_runs:
        ve.tensor_copy(T.b0[:, dst:dst + w], T.bs[:, src:src + w]).then_inc(sem.ob0, 1)

    def ve_s(c):
        ve.wait_ge(sem["ps%d" % c], G)
        ve.tensor_scalar(T.ss[:, c * SW:(c + 1) * SW], bank[c][:, 0:SW], 0.0, None, vmax).then_inc(sem["vr%d" % c], 1)

    def ve_o(c):
        ve.wait_ge(sem["po%d" % c], G)
        ve.tensor_copy(T.og[:, (c - 1) * QP:c * QP], obank[c][:, 0:QP]).then_inc(sem["vc%d" % c], 1)

    ve_s(1)
    ve_s(2)
    ve_s(3)
    ve_o(1)
    ve_o(2)
    ve_o(3)
    ve_s(0)
    p = obank[0]
    ve.wait_ge(sem.po0, G)
    ve.wait_ge(sem.oi1, n_in[1])
    ve.tensor_tensor(p[:, QP:2 * QP], p[:, 0:QP], T.oi[:, 0:QP], add).then_inc(sem.a1, 1)
    ve.wait_ge(sem.a1, 1)
    ve.wait_ge(sem.oi2, n_in[2])
    ve.tensor_tensor(p[:, 2 * QP:3 * QP], p[:, QP:2 * QP], T.oi[:, QP:2 * QP], add).then_inc(sem.a2, 1)
    ve.wait_ge(sem.a2, 1)
    ve.wait_ge(sem.oi3, n_in[3])
    ve.tensor_tensor(T.ys[:, :], p[:, 2 * QP:3 * QP], T.oi[:, 2 * QP:3 * QP], add).then_inc(sem.vy, 1)

    g.sync.wait_ge(sem.vy, 1)
    g.sync.dma_start(T.y[:, :], T.ys[:, :]).then_inc(sem.st, 16)
    g.sync.wait_ge(sem.st, 16)
